import numpy as np
import ml_dtypes


def mxq(x, axis, fmt="e4m3"):
    dtype, down = {"e4m3": (ml_dtypes.float8_e4m3fn, 7), "e5m2": (ml_dtypes.float8_e5m2, 14)}[fmt]
    v = np.moveaxis(np.asarray(x, np.float32).astype(ml_dtypes.bfloat16).astype(np.float64), axis, -1)
    blocks = v.reshape(v.shape[:-1] + (-1, 32))
    amax = np.abs(blocks).max(-1, keepdims=True)
    byte = np.maximum(np.where(amax > 0, np.frexp(amax)[1] - 1 + 127, 0) - down, 1)
    scale = np.exp2(byte - 127.0)
    codes = (blocks / scale).astype(np.float32).astype(dtype).astype(np.float64)
    return np.moveaxis((codes * scale).reshape(v.shape), -1, axis)


WIDE = False


def mx_kscale(k):
    if not WIDE:
        return np.ones(k)
    levels = np.array([10, -10, 5, -5, 0])
    if k % 512:
        return np.exp2(np.random.permutation(np.resize(levels, k // 32))).repeat(32)
    a = np.empty((k // 512, 16))
    for p in range(k // 512):
        a[p, :8] = np.random.permutation(np.resize(levels, 8))
        for g in range(8):
            far = levels[np.abs(levels - a[p, g]) >= 10]
            a[p, g + 8] = far[np.random.randint(len(far))]
    return np.exp2(a.ravel()).repeat(32)


def f64(x):
    return np.asarray(x).astype(np.float64)


def striped(idx):
    return np.tile(idx.reshape(-1, 16).T, (8, 1)).astype(np.uint16)


def unstriped(offs):
    return offs[:16].T.reshape(-1).astype(np.int64)

def planes(y):
    n, m = y.shape
    v = y.astype(np.float32).astype(ml_dtypes.bfloat16).astype(np.float64).reshape(n // 32, 32, m)
    top = np.abs(v).max(1)
    byte = np.clip(np.where(top > 0, np.frexp(top)[1] - 1 + 127 - 7, 1), 1, 254)
    codes = (v * np.exp2(127.0 - byte)[:, None, :]).reshape(n, m).astype(np.float32).astype(ml_dtypes.float8_e4m3fn).view(np.uint8)
    words = codes.reshape(n // 512, 128, 4, m).transpose(0, 1, 3, 2)
    return np.ascontiguousarray(words), np.ascontiguousarray(byte.astype(np.uint8).reshape(n // 512, 16, m))


K, T, S, H = 512, 1024, 512, 512


def setup_inputs():
    n = np.random.standard_normal
    s = mx_kscale(K)[:, None]
    u = mx_kscale(H)
    return {
        "xT": (n((K, T)) * s).astype(np.float32),
        "w1": (n((K, H)) / np.sqrt(K) / s * u).astype(np.float32),
        "w2": (n((H, H)) / np.sqrt(H) / u[:, None]).astype(np.float32),
        "offs": striped(np.random.permutation(T)[:S]),
    }


def reference(xT, w1, w2, offs):
    xq = mxq(f64(xT)[:, unstriped(offs)], 0, "e4m3")
    h = mxq(f64(w1), 0, "e4m3").T @ xq
    z = h - h.mean(axis=1, keepdims=True)
    out_0 = mxq(f64(w2), 0, "e4m3").T @ mxq(z, 0, "e4m3")
    return (out_0,) + planes(out_0)

@@ -1,0 +1,198 @@
+from contextlib import ExitStack
+
+import concourse.mybir as mybir
+
+K, T, S, H = 512, 1024, 512, 512
+FLOPS = 2 * K * H * S + 2 * H * H * S
+
+F32 = mybir.dt.float32
+BF16 = mybir.dt.bfloat16
+U32 = mybir.dt.uint32
+I32 = mybir.dt.int32
+U16 = mybir.dt.uint16
+U8 = mybir.dt.uint8
+FP8X4 = mybir.dt.float8_e4m3fn_x4
+COPY = mybir.ActivationFunctionType.Copy
+MULT = mybir.AluOpType.mult
+ADD = mybir.AluOpType.add
+
+P = 128
+PACK = 4
+HALF = S // 2
+BLOCK = 128
+BLOCKS = S // BLOCK
+LIST = 16
+VECTOR_SHARE = 88
+VECTOR_TOKENS = 256
+
+
+def quantize(nc, words, scales, grouped):
+    nc.vector.quantize_mx(out=words.bitcast(FP8X4), scales=scales, in_=grouped)
+
+
+def interleave(copy, grouped, planes, t0=0, t1=PACK):
+    copy(
+        out=grouped.rearrange("p (c i t) -> p c t i", i=4, t=PACK)[:, :, t0:t1, :],
+        in_=planes.rearrange("p t (c i) -> p c t i", i=4)[:, :, t0:t1, :],
+    )
+
+
+def deal_weights(copy, grouped, raw, pair, m0, m1):
+    copy(
+        out=grouped[:].rearrange("p (t m j) -> p m t j", t=PACK, j=PACK)[:, m0:m1, :, 2 * pair : 2 * pair + 2],
+        in_=raw[:].rearrange("p j (m t) -> p m t j", t=PACK)[:, m0:m1, :, :],
+    )
+
+
+def deal_columns(copy, grouped, raw, half):
+    copy(
+        out=grouped[:].rearrange("p (t m j) -> p m j t", t=PACK, j=PACK)[:, 64 * half : 64 * (half + 1), :, :],
+        in_=raw[:].rearrange("p j (m t) -> p m j t", t=PACK),
+    )
+
+
+def tile_picked_deepset_none_lo_kernel(tc, xT, w1, w2, offs, out_0, out_1, out_2):
+    nc = tc.nc
+    vcopy, scopy = nc.vector.tensor_copy, nc.scalar.copy
+
+    with ExitStack() as ctx:
+        keep = ctx.enter_context(tc.tile_pool(name="keep", bufs=1))
+        psum = ctx.enter_context(tc.psum_pool(name="psum", bufs=1))
+
+        def tile(shape, dtype, name, tag=None):
+            return keep.tile(shape, dtype, name=name, tag=tag or name, align_bytes=64)
+
+        offsets = keep.tile([P, S // LIST], U16, name="offsets")
+
+        x_rows = xT.rearrange("(p j) c -> p j c", j=PACK)
+        x_plane = [tile([P, T], F32, f"x_plane{j}") for j in range(PACK)]
+        for j in range(PACK):
+            nc.sync.dma_start(x_plane[j][:], x_rows[:, j, :])
+            if j == 0:
+                nc.sync.dma_start(offsets[:], offs)
+        w1_rows = w1.rearrange("(p j) c -> p j c", j=PACK)
+        w1_raw = [tile([P, 2, H], F32, f"w1_raw{pair}") for pair in range(2)]
+        for pair in range(2):
+            nc.sync.dma_start(w1_raw[pair][:], w1_rows[:, 2 * pair : 2 * pair + 2, :])
+        w2_rows = w2.rearrange("(p j) c -> p j c", j=PACK)
+        w2_raw = [tile([P, PACK, H // 2], F32, f"w2_raw{half}") for half in range(2)]
+        for half in range(2):
+            nc.sync.dma_start(w2_raw[half][:], w2_rows[:, :, H // 2 * half : H // 2 * (half + 1)])
+
+        x_grouped = tile([P, S * PACK], BF16, "x_grouped")
+        x_picked = tile([P, PACK, S - VECTOR_TOKENS], BF16, "x_picked")
+        x_scales = [tile([P, HALF], U8, f"x_scales{h}") for h in range(2)]
+        first, second = offsets[:, 0 : VECTOR_TOKENS // LIST], offsets[:, VECTOR_TOKENS // LIST : S // LIST]
+        for j in range(PACK):
+            vcopy(
+                out=x_grouped[:].rearrange("p (c j) -> p c j", j=PACK)[:, 0:VECTOR_TOKENS, j],
+                in_=x_plane[j][:].indirect(first),
+            )
+            nc.scalar.activation(out=x_picked[:, j, :], in_=x_plane[j][:].indirect(second), func=COPY)
+            if j % 2 == 1:
+                interleave(scopy, x_grouped[:, PACK * VECTOR_TOKENS : PACK * S], x_picked[:], j - 1, j + 1)
+        x_words = [tile([P, HALF], U32, "x_words0")]
+        quantize(nc, x_words[0][:], x_scales[0][:], x_grouped[:, 0 : PACK * HALF])
+
+        w1_grouped = tile([P, H * PACK], BF16, "w1_grouped")
+        w1_words = tile([P, H], U32, "w1_words")
+        w1_scales = tile([P, H], U8, "w1_scales")
+        deal_weights(vcopy, w1_grouped, w1_raw[0], 0, 0, P)
+        deal_weights(vcopy, w1_grouped, w1_raw[1], 1, 0, VECTOR_SHARE)
+        deal_weights(scopy, w1_grouped, w1_raw[1], 1, VECTOR_SHARE, P)
+        x_words.append(tile([P, HALF], U32, "x_words1", tag="w1_raw1"))
+        quantize(nc, x_words[1][:], x_scales[1][:], x_grouped[:, PACK * HALF : PACK * S])
+
+        h_bank = [psum.tile([P, S], F32, name=f"h_bank{t}") for t in range(PACK)]
+        quantize(nc, w1_words[:, 0:P], w1_scales[:, 0:P], w1_grouped[:, 0 : PACK * P])
+        quantize(nc, w1_words[:, P:H], w1_scales[:, P:H], w1_grouped[:, PACK * P : PACK * H])
+        for t in range(PACK):
+            cols = slice(P * t, P * (t + 1))
+            for h in range(2):
+                nc.tensor.matmul_mx(
+                    out=h_bank[t][:, HALF * h : HALF * (h + 1)],
+                    lhsT=w1_words[:, cols].bitcast(FP8X4),
+                    lhsT_scale=w1_scales[:, cols],
+                    rhs=x_words[h][:].bitcast(FP8X4),
+                    rhs_scale=x_scales[h][:],
+                    start=True,
+                    stop=True,
+                )
+
+        w2_grouped = tile([P, H * PACK], BF16, "w2_grouped")
+        w2_words = tile([P, H], U32, "w2_words")
+        w2_scales = tile([P, H], U8, "w2_scales")
+
+        deal_columns(scopy, w2_grouped, w2_raw[0], 0)
+        deal_columns(vcopy, w2_grouped, w2_raw[1], 1)
+        quantize(nc, w2_words[:], w2_scales[:], w2_grouped[:])
+
+        h_scaled = [tile([P, S], F32, f"h_scaled{t}") for t in range(PACK)]
+        minus_mean = [tile([P, 1], F32, f"minus_mean{t}") for t in range(PACK)]
+        z_planes = tile([P, PACK, S], BF16, "z_planes")
+        for t in range(PACK):
+            nc.scalar.activation(
+                out=h_scaled[t][:], in_=h_bank[t][:], func=COPY, scale=-1.0 / S, accum_out=minus_mean[t][:]
+            )
+
+        z_grouped = [tile([P, BLOCK * PACK], BF16, f"z_grouped{b}") for b in range(BLOCKS)]
+
+        def centre(out, t, cols):
+            nc.vector.tensor_scalar(
+                out=out,
+                in0=h_scaled[t][:, cols],
+                scalar1=-float(S),
+                scalar2=minus_mean[t][:],
+                op0=MULT,
+                op1=ADD,
+            )
+
+        for t in range(PACK - 1):
+            centre(z_planes[:, t, :], t, slice(0, S))
+        interleave(vcopy, z_grouped[0][:], z_planes[:, :, 0:BLOCK], 0, PACK - 1)
+        centre(z_grouped[0][:].rearrange("p (c t) -> p c t", t=PACK)[:, :, PACK - 1], PACK - 1, slice(0, BLOCK))
+        centre(z_planes[:, PACK - 1, BLOCK:S], PACK - 1, slice(BLOCK, S))
+
+        z_words = tile([P, S], U32, "z_words")
+        z_scales = tile([P, S], U8, "z_scales")
+        y_words = tile([P, S], U32, "y_words")
+        y_scales = tile([P, S], U8, "y_scales")
+        y_rows = out_0.rearrange("(p t) c -> p t c", t=PACK)
+        words_out = out_1[0].rearrange("p c r -> p (c r)").bitcast(I32)
+        scales_out = out_2[0].bitcast(I32)
+        y_bank = [psum.tile([P, PACK, BLOCK], F32, name=f"y_bank{b}") for b in range(BLOCKS)]
+        y_last = psum.tile([P, 2, BLOCK], F32, name="y_last", tag="h_bank0")
+        for b in range(BLOCKS):
+            cols = slice(BLOCK * b, BLOCK * (b + 1))
+            if b > 0:
+                interleave(scopy if b == 1 else vcopy, z_grouped[b][:], z_planes[:, :, cols])
+            quantize(nc, z_words[:, cols], z_scales[:, cols], z_grouped[b][:])
+            for t in range(PACK):
+                w_cols = slice(P * t, P * (t + 1))
+                nc.tensor.matmul_mx(
+                    out=y_last[:, t - 2, :] if b == BLOCKS - 1 and t >= 2 else y_bank[b][:, t, :],
+                    lhsT=w2_words[:, w_cols].bitcast(FP8X4),
+                    lhsT_scale=w2_scales[:, w_cols],
+                    rhs=z_words[:, cols].bitcast(FP8X4),
+                    rhs_scale=z_scales[:, cols],
+                    start=True,
+                    stop=True,
+                )
+        for b in range(BLOCKS):
+            cols = slice(BLOCK * b, BLOCK * (b + 1))
+            y = tile([P, PACK, BLOCK], F32, f"y{b}")
+            y_grouped = tile([P, BLOCK * PACK], BF16, f"y_grouped{b}")
+            if b < BLOCKS - 1:
+                scopy(out=y[:], in_=y_bank[b][:])
+            else:
+                scopy(out=y[:, 0:2, :], in_=y_bank[b][:, 0:2, :])
+                vcopy(out=y[:, 2:4, :], in_=y_last[:])
+            nc.sync.dma_start(y_rows[:, :, cols], y[:])
+            interleave(vcopy, y_grouped[:], y[:])
+            quantize(nc, y_words[:, cols], y_scales[:, cols], y_grouped[:])
+            if b % 2 == 1:
+                both = slice(BLOCK * (b - 1), BLOCK * (b + 1))
+                nc.sync.dma_start(words_out[:, both], y_words[:, both].bitcast(I32))
+        for q in range(4):
+            queue = nc.sync if q % 2 == 0 else nc.scalar
+            queue.dma_start(scales_out[4 * q : 4 * q + 4, :], y_scales[32 * q : 32 * q + 4, :].bitcast(I32))

@@ -64,6 +64,10 @@ def tile_picked_deepset_none_lo_kernel(tc, xT, w1, w2, offs, out_0, out_1, out_2
 
         offsets = keep.tile([P, S // LIST], U16, name="offsets")
 
+        warm = tile([P, 2], F32, "warm")
+        nc.vector.memset(warm[:, 0:1], 0.0)
+        nc.scalar.activation(out=warm[:, 1:2], in_=warm[:, 0:1], func=COPY)
+
         x_rows = xT.rearrange("(p j) c -> p j c", j=PACK)
         x_plane = [tile([P, T], F32, f"x_plane{j}") for j in range(PACK)]
         for j in range(PACK):

@@ -13,6 +13,7 @@ U16 = mybir.dt.uint16
 U8 = mybir.dt.uint8
 FP8X4 = mybir.dt.float8_e4m3fn_x4
 COPY = mybir.ActivationFunctionType.Copy
+IDENTITY = mybir.ActivationFunctionType.Identity
 MULT = mybir.AluOpType.mult
 ADD = mybir.AluOpType.add
 
@@ -37,17 +38,17 @@ def interleave(copy, grouped, planes, t0=0, t1=PACK):
     )
 
 
-def deal_weights(copy, grouped, raw, pair, m0, m1):
+def deal_weights(copy, grouped, raw, pair, m0, m1, base=0):
     copy(
         out=grouped[:].rearrange("p (t m j) -> p m t j", t=PACK, j=PACK)[:, m0:m1, :, 2 * pair : 2 * pair + 2],
-        in_=raw[:].rearrange("p j (m t) -> p m t j", t=PACK)[:, m0:m1, :, :],
+        in_=raw[:].rearrange("p j (m t) -> p m t j", t=PACK)[:, m0 - base : m1 - base, :, :],
     )
 
 
-def deal_columns(copy, grouped, raw, half):
+def deal_columns(copy, grouped, raw, half, m0, m1):
     copy(
-        out=grouped[:].rearrange("p (t m j) -> p m j t", t=PACK, j=PACK)[:, 64 * half : 64 * (half + 1), :, :],
-        in_=raw[:].rearrange("p j (m t) -> p m j t", t=PACK),
+        out=grouped[:].rearrange("p (t m j) -> p m j t", t=PACK, j=PACK)[:, 64 * half + m0 : 64 * half + m1, :, :],
+        in_=raw[:].rearrange("p j (m t) -> p m j t", t=PACK)[:, m0:m1, :, :],
     )
 
 
@@ -75,9 +76,10 @@ def tile_picked_deepset_none_lo_kernel(tc, xT, w1, w2, offs, out_0, out_1, out_2
             if j == 0:
                 nc.sync.dma_start(offsets[:], offs)
         w1_rows = w1.rearrange("(p j) c -> p j c", j=PACK)
-        w1_raw = [tile([P, 2, H], F32, f"w1_raw{pair}") for pair in range(2)]
-        for pair in range(2):
-            nc.sync.dma_start(w1_raw[pair][:], w1_rows[:, 2 * pair : 2 * pair + 2, :])
+        w1_pieces = [(0, 0, P), (1, 0, 96), (1, 96, P)]
+        w1_raw = [tile([P, 2, PACK * (m1 - m0)], F32, f"w1_raw{n}") for n, (pair, m0, m1) in enumerate(w1_pieces)]
+        for raw, (pair, m0, m1) in zip(w1_raw, w1_pieces):
+            nc.sync.dma_start(raw[:], w1_rows[:, 2 * pair : 2 * pair + 2, PACK * m0 : PACK * m1])
         w2_rows = w2.rearrange("(p j) c -> p j c", j=PACK)
         w2_raw = [tile([P, PACK, H // 2], F32, f"w2_raw{half}") for half in range(2)]
         for half in range(2):
@@ -102,14 +104,16 @@ def tile_picked_deepset_none_lo_kernel(tc, xT, w1, w2, offs, out_0, out_1, out_2
         w1_words = tile([P, H], U32, "w1_words")
         w1_scales = tile([P, H], U8, "w1_scales")
         deal_weights(vcopy, w1_grouped, w1_raw[0], 0, 0, P)
-        deal_weights(vcopy, w1_grouped, w1_raw[1], 1, 0, VECTOR_SHARE)
-        deal_weights(scopy, w1_grouped, w1_raw[1], 1, VECTOR_SHARE, P)
-        x_words.append(tile([P, HALF], U32, "x_words1", tag="w1_raw1"))
+        deal_weights(vcopy, w1_grouped, w1_raw[1], 1, 0, 68)
+        deal_weights(scopy, w1_grouped, w1_raw[1], 1, 68, 96)
+        deal_weights(vcopy, w1_grouped, w1_raw[2], 1, 96, 116, 96)
+        deal_weights(scopy, w1_grouped, w1_raw[2], 1, 116, P, 96)
+        x_words.append(tile([P, HALF], U32, "x_words1", tag="w1_raw2"))
         quantize(nc, x_words[1][:], x_scales[1][:], x_grouped[:, PACK * HALF : PACK * S])
 
         h_bank = [psum.tile([P, S], F32, name=f"h_bank{t}") for t in range(PACK)]
-        quantize(nc, w1_words[:, 0:P], w1_scales[:, 0:P], w1_grouped[:, 0 : PACK * P])
-        quantize(nc, w1_words[:, P:H], w1_scales[:, P:H], w1_grouped[:, PACK * P : PACK * H])
+        for t0, t1 in ((0, 1), (1, 2), (2, 4)):
+            quantize(nc, w1_words[:, P * t0 : P * t1], w1_scales[:, P * t0 : P * t1], w1_grouped[:, PACK * P * t0 : PACK * P * t1])
         for t in range(PACK):
             cols = slice(P * t, P * (t + 1))
             for h in range(2):
@@ -127,8 +131,9 @@ def tile_picked_deepset_none_lo_kernel(tc, xT, w1, w2, offs, out_0, out_1, out_2
         w2_words = tile([P, H], U32, "w2_words")
         w2_scales = tile([P, H], U8, "w2_scales")
 
-        deal_columns(scopy, w2_grouped, w2_raw[0], 0)
-        deal_columns(vcopy, w2_grouped, w2_raw[1], 1)
+        deal_columns(scopy, w2_grouped, w2_raw[0], 0, 0, 40)
+        deal_columns(vcopy, w2_grouped, w2_raw[0], 0, 40, 64)
+        deal_columns(vcopy, w2_grouped, w2_raw[1], 1, 0, 64)
         quantize(nc, w2_words[:], w2_scales[:], w2_grouped[:])
 
         h_scaled = [tile([P, S], F32, f"h_scaled{t}") for t in range(PACK)]
@@ -151,11 +156,19 @@ def tile_picked_deepset_none_lo_kernel(tc, xT, w1, w2, offs, out_0, out_1, out_2
                 op1=ADD,
             )
 
-        for t in range(PACK - 1):
+        for t in range(PACK - 2):
             centre(z_planes[:, t, :], t, slice(0, S))
+        centre(z_planes[:, PACK - 2, 0:BLOCK], PACK - 2, slice(0, BLOCK))
+        centre(z_planes[:, PACK - 2, BLOCK:S], PACK - 2, slice(BLOCK, S))
         interleave(vcopy, z_grouped[0][:], z_planes[:, :, 0:BLOCK], 0, PACK - 1)
         centre(z_grouped[0][:].rearrange("p (c t) -> p c t", t=PACK)[:, :, PACK - 1], PACK - 1, slice(0, BLOCK))
-        centre(z_planes[:, PACK - 1, BLOCK:S], PACK - 1, slice(BLOCK, S))
+        nc.scalar.activation(
+            out=z_planes[:, PACK - 1, BLOCK:S],
+            in_=h_scaled[PACK - 1][:, BLOCK:S],
+            func=IDENTITY,
+            scale=-float(S),
+            bias=minus_mean[PACK - 1][:],
+        )
 
         z_words = tile([P, S], U32, "z_words")
         z_scales = tile([P, S], U8, "z_scales")
@@ -169,7 +182,7 @@ def tile_picked_deepset_none_lo_kernel(tc, xT, w1, w2, offs, out_0, out_1, out_2
         for b in range(BLOCKS):
             cols = slice(BLOCK * b, BLOCK * (b + 1))
             if b > 0:
-                interleave(scopy if b == 1 else vcopy, z_grouped[b][:], z_planes[:, :, cols])
+                interleave(scopy if b == 2 else vcopy, z_grouped[b][:], z_planes[:, :, cols])
             quantize(nc, z_words[:, cols], z_scales[:, cols], z_grouped[b][:])
             for t in range(PACK):
                 w_cols = slice(P * t, P * (t + 1))
@@ -194,9 +207,9 @@ def tile_picked_deepset_none_lo_kernel(tc, xT, w1, w2, offs, out_0, out_1, out_2
             nc.sync.dma_start(y_rows[:, :, cols], y[:])
             interleave(vcopy, y_grouped[:], y[:])
             quantize(nc, y_words[:, cols], y_scales[:, cols], y_grouped[:])
-            if b % 2 == 1:
-                both = slice(BLOCK * (b - 1), BLOCK * (b + 1))
-                nc.sync.dma_start(words_out[:, both], y_words[:, both].bitcast(I32))
+            if b >= BLOCKS - 2:
+                done = slice(0 if b == BLOCKS - 2 else cols.start, cols.stop)
+                nc.sync.dma_start(words_out[:, done], y_words[:, done].bitcast(I32))
         for q in range(4):
             queue = nc.sync if q % 2 == 0 else nc.scalar
             queue.dma_start(scales_out[4 * q : 4 * q + 4, :], y_scales[32 * q : 32 * q + 4, :].bitcast(I32))

from contextlib import ExitStack

import concourse.mybir as mybir

K, T, S, H = 512, 1024, 512, 512
FLOPS = 2 * K * H * S + 2 * H * H * S

F32 = mybir.dt.float32
BF16 = mybir.dt.bfloat16
U32 = mybir.dt.uint32
I32 = mybir.dt.int32
U16 = mybir.dt.uint16
U8 = mybir.dt.uint8
FP8X4 = mybir.dt.float8_e4m3fn_x4
COPY = mybir.ActivationFunctionType.Copy
IDENTITY = mybir.ActivationFunctionType.Identity
MULT = mybir.AluOpType.mult
ADD = mybir.AluOpType.add

P = 128
PACK = 4
HALF = S // 2
BLOCK = 128
BLOCKS = S // BLOCK
LIST = 16
VECTOR_SHARE = 88
VECTOR_TOKENS = 256


def quantize(nc, words, scales, grouped):
    nc.vector.quantize_mx(out=words.bitcast(FP8X4), scales=scales, in_=grouped)


def interleave(copy, grouped, planes, t0=0, t1=PACK):
    copy(
        out=grouped.rearrange("p (c i t) -> p c t i", i=4, t=PACK)[:, :, t0:t1, :],
        in_=planes.rearrange("p t (c i) -> p c t i", i=4)[:, :, t0:t1, :],
    )


def deal_weights(copy, grouped, raw, pair, m0, m1, base=0):
    copy(
        out=grouped[:].rearrange("p (t m j) -> p m t j", t=PACK, j=PACK)[:, m0:m1, :, 2 * pair : 2 * pair + 2],
        in_=raw[:].rearrange("p j (m t) -> p m t j", t=PACK)[:, m0 - base : m1 - base, :, :],
    )


def deal_columns(copy, grouped, raw, half, m0, m1):
    copy(
        out=grouped[:].rearrange("p (t m j) -> p m j t", t=PACK, j=PACK)[:, 64 * half + m0 : 64 * half + m1, :, :],
        in_=raw[:].rearrange("p j (m t) -> p m j t", t=PACK)[:, m0:m1, :, :],
    )


def tile_picked_deepset_none_lo_kernel(tc, xT, w1, w2, offs, out_0, out_1, out_2):
    nc = tc.nc
    vcopy, scopy = nc.vector.tensor_copy, nc.scalar.copy

    with ExitStack() as ctx:
        keep = ctx.enter_context(tc.tile_pool(name="keep", bufs=1))
        psum = ctx.enter_context(tc.psum_pool(name="psum", bufs=1))

        def tile(shape, dtype, name, tag=None):
            return keep.tile(shape, dtype, name=name, tag=tag or name, align_bytes=64)

        offsets = keep.tile([P, S // LIST], U16, name="offsets")

        warm = tile([P, 2], F32, "warm")
        nc.vector.memset(warm[:, 0:1], 0.0)
        nc.scalar.activation(out=warm[:, 1:2], in_=warm[:, 0:1], func=COPY)

        x_rows = xT.rearrange("(p j) c -> p j c", j=PACK)
        x_plane = [tile([P, T], F32, f"x_plane{j}") for j in range(PACK)]
        for j in range(PACK):
            nc.sync.dma_start(x_plane[j][:], x_rows[:, j, :])
            if j == 0:
                nc.sync.dma_start(offsets[:], offs)
        w1_rows = w1.rearrange("(p j) c -> p j c", j=PACK)
        w1_pieces = [(0, 0, P), (1, 0, 96), (1, 96, P)]
        w1_raw = [tile([P, 2, PACK * (m1 - m0)], F32, f"w1_raw{n}") for n, (pair, m0, m1) in enumerate(w1_pieces)]
        for raw, (pair, m0, m1) in zip(w1_raw, w1_pieces):
            nc.sync.dma_start(raw[:], w1_rows[:, 2 * pair : 2 * pair + 2, PACK * m0 : PACK * m1])
        w2_rows = w2.rearrange("(p j) c -> p j c", j=PACK)
        w2_raw = [tile([P, PACK, H // 2], F32, f"w2_raw{half}") for half in range(2)]
        for half in range(2):
            nc.sync.dma_start(w2_raw[half][:], w2_rows[:, :, H // 2 * half : H // 2 * (half + 1)])

        x_grouped = tile([P, S * PACK], BF16, "x_grouped")
        x_picked = tile([P, PACK, S - VECTOR_TOKENS], BF16, "x_picked")
        x_scales = [tile([P, HALF], U8, f"x_scales{h}") for h in range(2)]
        first, second = offsets[:, 0 : VECTOR_TOKENS // LIST], offsets[:, VECTOR_TOKENS // LIST : S // LIST]
        for j in range(PACK):
            vcopy(
                out=x_grouped[:].rearrange("p (c j) -> p c j", j=PACK)[:, 0:VECTOR_TOKENS, j],
                in_=x_plane[j][:].indirect(first),
            )
            nc.scalar.activation(out=x_picked[:, j, :], in_=x_plane[j][:].indirect(second), func=COPY)
            if j % 2 == 1:
                interleave(scopy, x_grouped[:, PACK * VECTOR_TOKENS : PACK * S], x_picked[:], j - 1, j + 1)
        x_words = [tile([P, HALF], U32, "x_words0")]
        quantize(nc, x_words[0][:], x_scales[0][:], x_grouped[:, 0 : PACK * HALF])

        w1_grouped = tile([P, H * PACK], BF16, "w1_grouped")
        w1_words = tile([P, H], U32, "w1_words")
        w1_scales = tile([P, H], U8, "w1_scales")
        deal_weights(vcopy, w1_grouped, w1_raw[0], 0, 0, P)
        deal_weights(vcopy, w1_grouped, w1_raw[1], 1, 0, 68)
        deal_weights(scopy, w1_grouped, w1_raw[1], 1, 68, 96)
        deal_weights(vcopy, w1_grouped, w1_raw[2], 1, 96, 116, 96)
        deal_weights(scopy, w1_grouped, w1_raw[2], 1, 116, P, 96)
        x_words.append(tile([P, HALF], U32, "x_words1", tag="w1_raw2"))
        quantize(nc, x_words[1][:], x_scales[1][:], x_grouped[:, PACK * HALF : PACK * S])

        h_bank = [psum.tile([P, S], F32, name=f"h_bank{t}") for t in range(PACK)]
        for t0, t1 in ((0, 1), (1, 2), (2, 4)):
            quantize(nc, w1_words[:, P * t0 : P * t1], w1_scales[:, P * t0 : P * t1], w1_grouped[:, PACK * P * t0 : PACK * P * t1])
        for t in range(PACK):
            cols = slice(P * t, P * (t + 1))
            for h in range(2):
                nc.tensor.matmul_mx(
                    out=h_bank[t][:, HALF * h : HALF * (h + 1)],
                    lhsT=w1_words[:, cols].bitcast(FP8X4),
                    lhsT_scale=w1_scales[:, cols],
                    rhs=x_words[h][:].bitcast(FP8X4),
                    rhs_scale=x_scales[h][:],
                    start=True,
                    stop=True,
                )

        w2_grouped = tile([P, H * PACK], BF16, "w2_grouped")
        w2_words = tile([P, H], U32, "w2_words")
        w2_scales = tile([P, H], U8, "w2_scales")

        deal_columns(scopy, w2_grouped, w2_raw[0], 0, 0, 40)
        deal_columns(vcopy, w2_grouped, w2_raw[0], 0, 40, 64)
        deal_columns(vcopy, w2_grouped, w2_raw[1], 1, 0, 64)
        quantize(nc, w2_words[:], w2_scales[:], w2_grouped[:])

        h_scaled = [tile([P, S], F32, f"h_scaled{t}") for t in range(PACK)]
        minus_mean = [tile([P, 1], F32, f"minus_mean{t}") for t in range(PACK)]
        z_planes = tile([P, PACK, S], BF16, "z_planes")
        for t in range(PACK):
            nc.scalar.activation(
                out=h_scaled[t][:], in_=h_bank[t][:], func=COPY, scale=-1.0 / S, accum_out=minus_mean[t][:]
            )

        z_grouped = [tile([P, BLOCK * PACK], BF16, f"z_grouped{b}") for b in range(BLOCKS)]

        def centre(out, t, cols):
            nc.vector.tensor_scalar(
                out=out,
                in0=h_scaled[t][:, cols],
                scalar1=-float(S),
                scalar2=minus_mean[t][:],
                op0=MULT,
                op1=ADD,
            )

        for t in range(PACK - 2):
            centre(z_planes[:, t, :], t, slice(0, S))
        centre(z_planes[:, PACK - 2, 0:BLOCK], PACK - 2, slice(0, BLOCK))
        centre(z_planes[:, PACK - 2, BLOCK:S], PACK - 2, slice(BLOCK, S))
        interleave(vcopy, z_grouped[0][:], z_planes[:, :, 0:BLOCK], 0, PACK - 1)
        centre(z_grouped[0][:].rearrange("p (c t) -> p c t", t=PACK)[:, :, PACK - 1], PACK - 1, slice(0, BLOCK))
        nc.scalar.activation(
            out=z_planes[:, PACK - 1, BLOCK:S],
            in_=h_scaled[PACK - 1][:, BLOCK:S],
            func=IDENTITY,
            scale=-float(S),
            bias=minus_mean[PACK - 1][:],
        )

        z_words = tile([P, S], U32, "z_words")
        z_scales = tile([P, S], U8, "z_scales")
        y_words = tile([P, S], U32, "y_words")
        y_scales = tile([P, S], U8, "y_scales")
        y_rows = out_0.rearrange("(p t) c -> p t c", t=PACK)
        words_out = out_1[0].rearrange("p c r -> p (c r)").bitcast(I32)
        scales_out = out_2[0].bitcast(I32)
        y_bank = [psum.tile([P, PACK, BLOCK], F32, name=f"y_bank{b}") for b in range(BLOCKS)]
        y_last = psum.tile([P, 2, BLOCK], F32, name="y_last", tag="h_bank0")
        for b in range(BLOCKS):
            cols = slice(BLOCK * b, BLOCK * (b + 1))
            if b > 0:
                interleave(scopy if b == 2 else vcopy, z_grouped[b][:], z_planes[:, :, cols])
            quantize(nc, z_words[:, cols], z_scales[:, cols], z_grouped[b][:])
            for t in range(PACK):
                w_cols = slice(P * t, P * (t + 1))
                nc.tensor.matmul_mx(
                    out=y_last[:, t - 2, :] if b == BLOCKS - 1 and t >= 2 else y_bank[b][:, t, :],
                    lhsT=w2_words[:, w_cols].bitcast(FP8X4),
                    lhsT_scale=w2_scales[:, w_cols],
                    rhs=z_words[:, cols].bitcast(FP8X4),
                    rhs_scale=z_scales[:, cols],
                    start=True,
                    stop=True,
                )
        for b in range(BLOCKS):
            cols = slice(BLOCK * b, BLOCK * (b + 1))
            y = tile([P, PACK, BLOCK], F32, f"y{b}")
            y_grouped = tile([P, BLOCK * PACK], BF16, f"y_grouped{b}")
            if b < BLOCKS - 1:
                scopy(out=y[:], in_=y_bank[b][:])
            else:
                scopy(out=y[:, 0:2, :], in_=y_bank[b][:, 0:2, :])
                vcopy(out=y[:, 2:4, :], in_=y_last[:])
            nc.sync.dma_start(y_rows[:, :, cols], y[:])
            interleave(vcopy, y_grouped[:], y[:])
            quantize(nc, y_words[:, cols], y_scales[:, cols], y_grouped[:])
            if b >= BLOCKS - 2:
                done = slice(0 if b == BLOCKS - 2 else cols.start, cols.stop)
                nc.sync.dma_start(words_out[:, done], y_words[:, done].bitcast(I32))
        for q in range(4):
            queue = nc.sync if q % 2 == 0 else nc.scalar
            queue.dma_start(scales_out[4 * q : 4 * q + 4, :], y_scales[32 * q : 32 * q + 4, :].bitcast(I32))
